import numpy as np
import ml_dtypes


def mxq(x, axis, fmt="e4m3"):
    dtype, down = {"e4m3": (ml_dtypes.float8_e4m3fn, 7), "e5m2": (ml_dtypes.float8_e5m2, 14)}[fmt]
    v = np.moveaxis(np.asarray(x, np.float32).astype(ml_dtypes.bfloat16).astype(np.float64), axis, -1)
    blocks = v.reshape(v.shape[:-1] + (-1, 32))
    amax = np.abs(blocks).max(-1, keepdims=True)
    byte = np.maximum(np.where(amax > 0, np.frexp(amax)[1] - 1 + 127, 0) - down, 1)
    scale = np.exp2(byte - 127.0)
    codes = (blocks / scale).astype(np.float32).astype(dtype).astype(np.float64)
    return np.moveaxis((codes * scale).reshape(v.shape), -1, axis)


WIDE = False


def mx_kscale(k):
    if not WIDE:
        return np.ones(k)
    levels = np.array([10, -10, 5, -5, 0])
    if k % 512:
        return np.exp2(np.random.permutation(np.resize(levels, k // 32))).repeat(32)
    a = np.empty((k // 512, 16))
    for p in range(k // 512):
        a[p, :8] = np.random.permutation(np.resize(levels, 8))
        for g in range(8):
            far = levels[np.abs(levels - a[p, g]) >= 10]
            a[p, g + 8] = far[np.random.randint(len(far))]
    return np.exp2(a.ravel()).repeat(32)


def f64(x):
    return np.asarray(x).astype(np.float64)


def striped(idx):
    return np.tile(np.asarray(idx).reshape(-1, 16).T, (8, 1)).astype(np.uint16)


def unstriped(offs):
    return offs[:16].T.reshape(-1).astype(np.int64)


E2M1 = np.array([0.0, 0.5, 1.0, 1.5, 2.0, 3.0, 4.0, 6.0, -0.0, -0.5, -1.0, -1.5, -2.0, -3.0, -4.0, -6.0])


def pack_weight(w, fmt):
    k, n = w.shape
    w = f64(np.asarray(w, np.float32).astype(ml_dtypes.bfloat16)).reshape(k // 32, 32, n)
    amax = np.abs(w).max(1)
    if fmt == "e4m3":
        byte = np.frexp(amax)[1] - 1 + 127 - 7
    else:
        mant, ex = np.frexp(amax / 6.0)
        byte = np.where(mant > 0.5, ex, ex - 1) + 127
    byte = np.clip(np.where(amax > 0, byte, 1), 1, 254)
    scaled = (w * np.exp2(127.0 - byte)[:, None, :]).reshape(k, n).astype(np.float32)
    by_word = np.ascontiguousarray(scaled.reshape(k // 512, 128, 4, n).transpose(0, 1, 3, 2))
    if fmt == "e4m3":
        words = by_word.astype(ml_dtypes.float8_e4m3fn).view(np.uint8)
    else:
        c = by_word.astype(ml_dtypes.float4_e2m1fn).view(np.uint8) & 0xF
        words = (c[..., 0::2] | (c[..., 1::2] << 4)).reshape(k // 512, 128, 2 * n)
    return np.ascontiguousarray(words), np.ascontiguousarray(byte.astype(np.uint8).reshape(k // 512, 16, n))


def unpack_weight(words, scales, fmt):
    g, _, n = scales.shape
    words = np.ascontiguousarray(words).reshape(g, 128, n, -1)
    if fmt == "e4m3":
        vals = words.view(ml_dtypes.float8_e4m3fn).astype(np.float64)
    else:
        nib = np.empty((g, 128, n, 4), np.uint8)
        nib[..., 0::2] = words & 0xF
        nib[..., 1::2] = words >> 4
        vals = E2M1[nib]
    vals = vals * np.repeat(np.exp2(scales.astype(np.float64) - 127.0), 8, axis=1)[..., None]
    return vals.transpose(0, 1, 3, 2).reshape(g * 512, n)


D, T, I, J, U, E, M = 512, 2048, 512, 256, 1024, 512, 1024


def setup_inputs():
    n = np.random.standard_normal
    idx = np.random.permutation(T)[:I]
    idx2 = np.random.permutation(U)[:J]
    idx3 = np.random.permutation(M)[:J]
    fd = mx_kscale(D)
    fi = mx_kscale(I)
    ti = np.ones(T)
    ti[idx] = fi
    keysp = pack_weight(n((D, T)) / fd[:, None], "e4m3")
    return {
        "keys_words": keysp[0],
        "keys_scales": keysp[1],
        "notes": (n((D, U)) * 1.0 / np.sqrt(D) * fd[:, None]).astype(np.float32),
        "rowf": (np.random.uniform(0.02, 0.08, (I, 1)) * fi[:, None]).astype(np.float32),
        "vals": (n((E, T)) / ti).astype(np.float32),
        "held": (n((E, M))).astype(np.float32),
        "hgain": np.tile(np.random.uniform(0.5, 2.0, M), (128, 1)).astype(np.float32),
        "offs": striped(idx),
        "offs2": striped(idx2),
        "offs3": striped(idx3),
    }


def reference(keys_words, keys_scales, notes, rowf, vals, held, hgain, offs, offs2, offs3):
    idx = unstriped(offs)
    idx2 = unstriped(offs2)
    idx3 = unstriped(offs3)
    keysu = unpack_weight(keys_words, keys_scales, "e4m3")
    keysidxg = keysu[:, idx]
    notesidx2q = mxq(f64(notes)[:, idx2], 0, "e4m3")
    g9 = keysidxg.T @ notesidx2q
    g0 = np.tanh(g9)
    gr1 = g0 * f64(rowf)
    vt1 = f64(vals)[:, idx].T
    vt1q = mxq(vt1, 0, "e4m3")
    gr1q = mxq(gr1, 0, "e4m3")
    o = vt1q.T @ gr1q
    y = f64(held)[:, idx3] + o * f64(hgain)[:1][:, idx3]
    return y

@@ -1,0 +1,205 @@
+from contextlib import ExitStack
+
+import concourse.mybir as mybir
+from concourse.masks import make_identity
+
+D, T, I, J, U, E, M = 512, 2048, 512, 256, 1024, 512, 1024
+FLOPS = 2 * D * I * J + 2 * I * E * J
+BYTES = D * T + 16 * T + 4 * (D * U + I + E * T + E * M + M + E * J) + 2 * 128 * (I + J + J) // 16
+
+F32 = mybir.dt.float32
+BF16 = mybir.dt.bfloat16
+I32 = mybir.dt.int32
+U32 = mybir.dt.uint32
+U16 = mybir.dt.uint16
+U8 = mybir.dt.uint8
+FP8X4 = mybir.dt.float8_e4m3fn_x4
+ACT = mybir.ActivationFunctionType
+ALU = mybir.AluOpType
+
+P = 128
+PACK = 4
+
+
+def tile_attend_tab_plain_merge_kernel(tc, keys_words, keys_scales, notes, rowf, vals, held, hgain, offs, offs2, offs3, out):
+    nc = tc.nc
+    with ExitStack() as ctx:
+        sb = ctx.enter_context(tc.tile_pool(name="sb", bufs=1))
+        both = ctx.enter_context(tc.tile_pool(name="both", bufs=1))
+        ps = ctx.enter_context(tc.psum_pool(name="ps", bufs=1))
+        ps2 = ctx.enter_context(tc.psum_pool(name="ps2", bufs=2))
+
+        idx = sb.tile([P, I // 16], U16, name="idx")
+        idx2 = sb.tile([P, J // 16], U16, name="idx2")
+        idx3 = sb.tile([P, J // 16], U16, name="idx3")
+        key_pool = sb.tile([P, T], U32, name="key_pool", tag="keys", align_bytes=64)
+        scale_pool = sb.tile([P, T], U8, name="scale_pool")
+        gain_pool = sb.tile([P, M], F32, name="gain_pool")
+        row_factor = sb.tile([P, PACK], F32, name="row_factor")
+        note_pool = [sb.tile([P, 2, U], F32, name=f"note_pool{a}", tag=f"notes{a}", align_bytes=64) for a in range(2)]
+        val_pool = [
+            both.tile([P, T], F32, name=f"val_pool{b}", offset=(0, 9216)[b - 2], align_bytes=64)
+            if b >= 2
+            else sb.tile([P, T], F32, name=f"val_pool{b}", tag=f"vals{b}", align_bytes=64)
+            for b in range(PACK)
+        ]
+        held_pool = [sb.tile([P, M], F32, name=f"held_pool{b}", tag=f"held{b}", align_bytes=64) for b in range(PACK)]
+        ident = sb.tile([P, P], F32, name="ident")
+
+        scale_rows = sb.tile([P, T // 4], I32, name="scale_rows")
+        gain_first = sb.tile([1, M], F32, name="gain_first")
+        nc.vector.memset(scale_pool[:].bitcast(I32), 0)
+        nc.gpsimd.memset(gain_pool[:], 0.0)
+        make_identity(nc, ident[:])
+
+        notes_v = notes.rearrange("(p t) u -> p t u", t=PACK)
+        vals_v = vals.rearrange("(p b) t -> p b t", b=PACK)
+        held_v = held.rearrange("(p b) m -> p b m", b=PACK)
+        out_v = out.rearrange("(p b) j -> p b j", b=PACK)
+
+        nc.sync.dma_start(idx2[:], offs2)
+        nc.sync.dma_start(idx[:], offs)
+        for a in range(2):
+            nc.sync.dma_start(note_pool[a][:], notes_v[:, 2 * a : 2 * a + 2, :])
+        nc.sync.dma_start(idx3[:], offs3)
+        nc.sync.dma_start(key_pool[:].bitcast(I32), keys_words[0].rearrange("p n r -> p (n r)").bitcast(I32))
+        for b in range(PACK):
+            nc.sync.dma_start(val_pool[b][:], vals_v[:, b, :])
+        for b in range(PACK):
+            nc.sync.dma_start(held_pool[b][:], held_v[:, b, :])
+        for q in range(4):
+            nc.scalar.dma_start(scale_rows[32 * q : 32 * q + 4, :], keys_scales[0, 4 * q : 4 * q + 4, :].bitcast(I32))
+        nc.scalar.dma_start(gain_first[:], hgain[0:1, :])
+        nc.scalar.dma_start(row_factor[:], rowf.rearrange("(p t) o -> p (t o)", t=PACK))
+
+        for q in range(4):
+            nc.vector.tensor_copy(scale_pool[32 * q : 32 * q + 4, :].bitcast(I32), scale_rows[32 * q : 32 * q + 4, :])
+        nc.scalar.activation(gain_pool[0:1, :], gain_first[:], ACT.Copy)
+
+        key_bytes = sb.tile([P, I], U8, name="key_bytes", align_bytes=64)
+        nc.vector.tensor_copy(key_bytes[:].rearrange("p (t s) -> p s t", t=PACK), scale_pool[:].indirect(idx[:]))
+
+        note_planes = sb.tile([P, 2, J], F32, name="note_planes")
+        note_bf = sb.tile([P, J, PACK], BF16, name="note_bf", align_bytes=64)
+        for t in range(2):
+            nc.scalar.activation(note_planes[:, t, :], note_pool[0][:, t, :].indirect(idx2[:]), ACT.Copy)
+        nc.scalar.activation(note_bf[:, :, 0:2], note_planes[:].rearrange("p t j -> p j t"), ACT.Copy)
+        for t in range(2):
+            nc.vector.tensor_copy(note_bf[:, :, 2 + t], note_pool[1][:, t, :].indirect(idx2[:]))
+        note_words = sb.tile([P, J], U32, name="note_words", align_bytes=64)
+        note_bytes = sb.tile([P, J], U8, name="note_bytes", align_bytes=64)
+        nc.vector.quantize_mx(note_words[:].bitcast(FP8X4), note_bytes[:], note_bf[:].rearrange("p j t -> p (j t)"))
+
+        key_words = sb.tile([P, I], U32, name="key_words", tag="notes1", align_bytes=64)
+        nc.vector.tensor_copy(key_words[:].rearrange("p (t s) -> p s t", t=PACK), key_pool[:].indirect(idx[:]))
+
+        gain_row = sb.tile([P, J], F32, name="gain_row")
+        nc.scalar.activation(gain_row[:], gain_pool[:].indirect(idx3[:]), ACT.Copy)
+        gain_turned = ps.tile([P, J // P, P], F32, name="gain_turned")
+        for h in range(J // P):
+            nc.tensor.transpose(gain_turned[:, h, :], gain_row[:, h * P : (h + 1) * P], ident[:])
+        gain_col = sb.tile([P, J // P], F32, name="gain_col")
+        nc.scalar.copy(gain_col[:], gain_turned[:, :, 0])
+        gain_spread = ps.tile([P, J // P, P], F32, name="gain_spread")
+        for h in range(J // P):
+            nc.tensor.transpose(gain_spread[:, h, :], gain_col[:, h : h + 1].to_broadcast([P, P]), ident[:])
+        gain = sb.tile([P, J], F32, name="gain", tag="gain", align_bytes=64)
+        nc.scalar.copy(gain[:], gain_spread[:].rearrange("p h j -> p (h j)"))
+
+        table_words = sb.tile([P, J], U32, name="table_words", align_bytes=64)
+        table_bytes = sb.tile([P, J], U8, name="table_bytes", align_bytes=64)
+        table_both = sb.tile([P, J // P, P, PACK], BF16, name="table_both", tag="vals0", align_bytes=64)
+        for h in range(J // P):
+            cols = slice(h * P, (h + 1) * P)
+            raw = ps.tile([P, PACK, P], F32, name=f"raw{h}")
+            for t in range(PACK):
+                rows = slice(t * P, (t + 1) * P)
+                nc.tensor.matmul_mx(
+                    raw[:, t, :],
+                    lhsT=key_words[:, rows].bitcast(FP8X4),
+                    lhsT_scale=key_bytes[:, rows],
+                    rhs=note_words[:, cols].bitcast(FP8X4),
+                    rhs_scale=note_bytes[:, cols],
+                    start=True,
+                    stop=True,
+                )
+            squashed = sb.tile([P, P, PACK], F32, name=f"squashed{h}", tag=f"squashed{h}", align_bytes=64)
+            nc.scalar.activation(squashed[:], raw[:].rearrange("p t j -> p j t"), ACT.Tanh)
+            table_bf = table_both[:, h]
+            nc.vector.tensor_tensor(
+                table_bf, squashed[:], row_factor[:].unsqueeze(1).to_broadcast([P, P, PACK]), ALU.mult
+            )
+            nc.vector.quantize_mx(
+                table_words[:, cols].bitcast(FP8X4), table_bytes[:, cols], table_bf.rearrange("p j t -> p (j t)")
+            )
+
+        last = PACK - 1
+
+        def turn(picked, val_bf):
+            pairs = picked[:].bitcast(F32)
+            turned = ps2.tile([P, 2, P], F32, name="turned")
+            for u in range(2):
+                nc.tensor.transpose(turned[:, u, :], pairs[:, u : I // 2 : 2], ident[:])
+            nc.vector.tensor_copy(val_bf.bitcast(F32), turned[:].rearrange("p u c -> p c u"))
+
+        def multiply(val_bf, blocks):
+            val_words = sb.tile([P, blocks * P], U32, name="val_words", bufs=3, align_bytes=64)
+            val_bytes = sb.tile([P, blocks * P], U8, name="val_bytes", bufs=3, align_bytes=64)
+            nc.vector.quantize_mx(val_words[:].bitcast(FP8X4), val_bytes[:], val_bf)
+            summed = ps2.tile([P, blocks, J], F32, name="summed")
+            for k in range(blocks):
+                nc.tensor.matmul_mx(
+                    summed[:, k, :],
+                    lhsT=val_words[:, k * P : (k + 1) * P].bitcast(FP8X4),
+                    lhsT_scale=val_bytes[:, k * P : (k + 1) * P],
+                    rhs=table_words[:].bitcast(FP8X4),
+                    rhs_scale=table_bytes[:],
+                    start=True,
+                    stop=True,
+                )
+            return summed
+
+        gained = []
+        for b in range(2):
+            picked = sb.tile([P, I], BF16, name=f"picked{b}", tag=("keys", "squashed0")[b], align_bytes=64)
+            if b == 0:
+                nc.vector.tensor_copy(picked[:], val_pool[b][:].indirect(idx[:]))
+                val_bf = sb.tile([P, P, PACK], BF16, name="val_bf0", align_bytes=64)
+            else:
+                nc.scalar.activation(picked[:], val_pool[b][:].indirect(idx[:]), ACT.Copy)
+                val_bf = both.tile([P, P, PACK], BF16, name="val_bf1", offset=8192, align_bytes=64)
+            turn(picked, val_bf[:])
+            summed = multiply(val_bf[:].rearrange("p c t -> p (c t)"), 1)
+            scaled = sb.tile([P, J], F32, name=f"gained{b}")
+            nc.vector.tensor_tensor(scaled[:], summed[:, 0, :], gain[:], ALU.mult)
+            gained.append(scaled)
+
+        picked2 = sb.tile([P, I], BF16, name="picked2", tag="vals1", align_bytes=64)
+        nc.scalar.activation(picked2[:], val_pool[2][:].indirect(idx[:]), ACT.Copy)
+        picked3 = both.tile([P, I], BF16, name="picked3", offset=8192 - I, align_bytes=64)
+        nc.vector.tensor_copy(picked3[:, : I // 2], val_pool[last][:].indirect(idx[:, : I // 32]))
+        nc.scalar.activation(picked3[:, I // 2 :], val_pool[last][:].indirect(idx[:, I // 32 :]), ACT.Copy)
+        val_bf23 = both.tile([P, 2, P, PACK], BF16, name="val_bf23", offset=9216, align_bytes=64)
+        turn(picked2, val_bf23[:, 0])
+        turn(picked3, val_bf23[:, 1])
+        summed23 = multiply(val_bf23[:].rearrange("p k c t -> p (k c t)"), 2)
+
+        looked = [
+            both.tile([P, J], F32, name="looked0", offset=9216 + 2048, align_bytes=64),
+            sb.tile([P, J], F32, name="looked1", tag="held0", align_bytes=64),
+            sb.tile([P, J], F32, name="looked2", tag="held1", align_bytes=64),
+        ]
+        for b in range(last):
+            nc.scalar.activation(looked[b][:], held_pool[b][:].indirect(idx3[:]), ACT.Copy)
+        first = both.tile([P, 2, J], F32, name="first", offset=9216, align_bytes=64)
+        for b in range(2):
+            nc.vector.tensor_tensor(first[:, b, :], looked[b][:], gained[b][:], ALU.add)
+        nc.sync.dma_start(out_v[:, 0:2, :], first[:])
+        gained23 = sb.tile([P, 2, J], F32, name="gained23", tag="held0", align_bytes=64)
+        nc.vector.tensor_tensor(gained23[:], summed23[:], gain[:].unsqueeze(1).to_broadcast([P, 2, J]), ALU.mult)
+        fourth = sb.tile([P, J], F32, name="fourth")
+        nc.vector.tensor_tensor(fourth[:], held_pool[last][:].indirect(idx3[:]), gained23[:, 1, :], ALU.add)
+        nc.sync.dma_start(out_v[:, last, :], fourth[:])
+        third = sb.tile([P, J], F32, name="third")
+        nc.vector.tensor_tensor(third[:], looked[2][:], gained23[:, 0, :], ALU.add)
+        nc.sync.dma_start(out_v[:, 2, :], third[:])

@@ -135,16 +135,16 @@ def tile_attend_tab_plain_merge_kernel(tc, keys_words, keys_scales, notes, rowf,
 
         last = PACK - 1
 
-        def turn(picked, val_bf):
+        def turn(picked, val_bf, copy):
             pairs = picked[:].bitcast(F32)
             turned = ps2.tile([P, 2, P], F32, name="turned")
             for u in range(2):
                 nc.tensor.transpose(turned[:, u, :], pairs[:, u : I // 2 : 2], ident[:])
-            nc.vector.tensor_copy(val_bf.bitcast(F32), turned[:].rearrange("p u c -> p c u"))
+            copy(val_bf.bitcast(F32), turned[:].rearrange("p u c -> p c u"))
 
         def multiply(val_bf, blocks):
-            val_words = sb.tile([P, blocks * P], U32, name="val_words", bufs=3, align_bytes=64)
-            val_bytes = sb.tile([P, blocks * P], U8, name="val_bytes", bufs=3, align_bytes=64)
+            val_words = sb.tile([P, blocks * P], U32, name="val_words", bufs=4, align_bytes=64)
+            val_bytes = sb.tile([P, blocks * P], U8, name="val_bytes", bufs=4, align_bytes=64)
             nc.vector.quantize_mx(val_words[:].bitcast(FP8X4), val_bytes[:], val_bf)
             summed = ps2.tile([P, blocks, J], F32, name="summed")
             for k in range(blocks):
@@ -168,7 +168,7 @@ def tile_attend_tab_plain_merge_kernel(tc, keys_words, keys_scales, notes, rowf,
             else:
                 nc.scalar.activation(picked[:], val_pool[b][:].indirect(idx[:]), ACT.Copy)
                 val_bf = both.tile([P, P, PACK], BF16, name="val_bf1", offset=8192, align_bytes=64)
-            turn(picked, val_bf[:])
+            turn(picked, val_bf[:], nc.vector.tensor_copy)
             summed = multiply(val_bf[:].rearrange("p c t -> p (c t)"), 1)
             scaled = sb.tile([P, J], F32, name=f"gained{b}")
             nc.vector.tensor_tensor(scaled[:], summed[:, 0, :], gain[:], ALU.mult)
@@ -177,12 +177,15 @@ def tile_attend_tab_plain_merge_kernel(tc, keys_words, keys_scales, notes, rowf,
         picked2 = sb.tile([P, I], BF16, name="picked2", tag="vals1", align_bytes=64)
         nc.scalar.activation(picked2[:], val_pool[2][:].indirect(idx[:]), ACT.Copy)
         picked3 = both.tile([P, I], BF16, name="picked3", offset=8192 - I, align_bytes=64)
-        nc.vector.tensor_copy(picked3[:, : I // 2], val_pool[last][:].indirect(idx[:, : I // 32]))
-        nc.scalar.activation(picked3[:, I // 2 :], val_pool[last][:].indirect(idx[:, I // 32 :]), ACT.Copy)
-        val_bf23 = both.tile([P, 2, P, PACK], BF16, name="val_bf23", offset=9216, align_bytes=64)
-        turn(picked2, val_bf23[:, 0])
-        turn(picked3, val_bf23[:, 1])
-        summed23 = multiply(val_bf23[:].rearrange("p k c t -> p (k c t)"), 2)
+        split = 320
+        nc.vector.tensor_copy(picked3[:, :split], val_pool[last][:].indirect(idx[:, : split // 16]))
+        nc.scalar.activation(picked3[:, split:], val_pool[last][:].indirect(idx[:, split // 16 :]), ACT.Copy)
+        val_bf2 = both.tile([P, P, PACK], BF16, name="val_bf2", offset=9216, align_bytes=64)
+        turn(picked2, val_bf2[:], nc.scalar.copy)
+        summed2 = multiply(val_bf2[:].rearrange("p c t -> p (c t)"), 1)
+        val_bf3 = sb.tile([P, P, PACK], BF16, name="val_bf3", tag="val_bf3", align_bytes=64)
+        turn(picked3, val_bf3[:], nc.vector.tensor_copy)
+        summed3 = multiply(val_bf3[:].rearrange("p c t -> p (c t)"), 1)
 
         looked = [
             both.tile([P, J], F32, name="looked0", offset=9216 + 2048, align_bytes=64),
@@ -191,15 +194,16 @@ def tile_attend_tab_plain_merge_kernel(tc, keys_words, keys_scales, notes, rowf,
         ]
         for b in range(last):
             nc.scalar.activation(looked[b][:], held_pool[b][:].indirect(idx3[:]), ACT.Copy)
-        first = both.tile([P, 2, J], F32, name="first", offset=9216, align_bytes=64)
+        first = sb.tile([P, 3, J], F32, name="first", tag="val_bf3", align_bytes=64)
+        nc.vector.tensor_tensor(first[:, 2, :], summed2[:, 0, :], gain[:], ALU.mult)
+        gained3 = sb.tile([P, J], F32, name="gained3")
+        nc.vector.tensor_tensor(gained3[:], summed3[:, 0, :], gain[:], ALU.mult)
         for b in range(2):
             nc.vector.tensor_tensor(first[:, b, :], looked[b][:], gained[b][:], ALU.add)
-        nc.sync.dma_start(out_v[:, 0:2, :], first[:])
-        gained23 = sb.tile([P, 2, J], F32, name="gained23", tag="held0", align_bytes=64)
-        nc.vector.tensor_tensor(gained23[:], summed23[:], gain[:].unsqueeze(1).to_broadcast([P, 2, J]), ALU.mult)
-        fourth = sb.tile([P, J], F32, name="fourth")
-        nc.vector.tensor_tensor(fourth[:], held_pool[last][:].indirect(idx3[:]), gained23[:, 1, :], ALU.add)
-        nc.sync.dma_start(out_v[:, last, :], fourth[:])
-        third = sb.tile([P, J], F32, name="third")
-        nc.vector.tensor_tensor(third[:], looked[2][:], gained23[:, 0, :], ALU.add)
+        nc.sync.dma_start(out_v[:, 0:2, :], first[:, 0:2, :])
+        third = sb.tile([P, J], F32, name="third", tag="gain", align_bytes=64)
+        nc.vector.tensor_tensor(third[:], looked[2][:], first[:, 2, :], ALU.add)
         nc.sync.dma_start(out_v[:, 2, :], third[:])
+        fourth = sb.tile([P, J], F32, name="fourth", tag="held1", align_bytes=64)
+        nc.vector.tensor_tensor(fourth[:], held_pool[last][:].indirect(idx3[:]), gained3[:], ALU.add)
+        nc.sync.dma_start(out_v[:, last, :], fourth[:])

@@ -38,7 +38,7 @@ def tile_attend_tab_plain_merge_kernel(tc, keys_words, keys_scales, notes, rowf,
         row_factor = sb.tile([P, PACK], F32, name="row_factor")
         note_pool = [sb.tile([P, 2, U], F32, name=f"note_pool{a}", tag=f"notes{a}", align_bytes=64) for a in range(2)]
         val_pool = [
-            both.tile([P, T], F32, name=f"val_pool{b}", offset=(0, 9216)[b - 2], align_bytes=64)
+            both.tile([P, T], F32, name=f"val_pool{b}", offset=(0, 10240)[b - 2], align_bytes=64)
             if b >= 2
             else sb.tile([P, T], F32, name=f"val_pool{b}", tag=f"vals{b}", align_bytes=64)
             for b in range(PACK)
@@ -86,7 +86,7 @@ def tile_attend_tab_plain_merge_kernel(tc, keys_words, keys_scales, notes, rowf,
         nc.scalar.activation(note_bf[:, :, 0:2], note_planes[:].rearrange("p t j -> p j t"), ACT.Copy)
         for t in range(2):
             nc.vector.tensor_copy(note_bf[:, :, 2 + t], note_pool[1][:, t, :].indirect(idx2[:]))
-        note_words = sb.tile([P, J], U32, name="note_words", align_bytes=64)
+        note_words = sb.tile([P, J], U32, name="note_words", tag="note_words", align_bytes=64)
         note_bytes = sb.tile([P, J], U8, name="note_bytes", align_bytes=64)
         nc.vector.quantize_mx(note_words[:].bitcast(FP8X4), note_bytes[:], note_bf[:].rearrange("p j t -> p (j t)"))
 
@@ -108,7 +108,7 @@ def tile_attend_tab_plain_merge_kernel(tc, keys_words, keys_scales, notes, rowf,
 
         table_words = sb.tile([P, J], U32, name="table_words", align_bytes=64)
         table_bytes = sb.tile([P, J], U8, name="table_bytes", align_bytes=64)
-        table_both = sb.tile([P, J // P, P, PACK], BF16, name="table_both", tag="vals0", align_bytes=64)
+        squashed = sb.tile([P, J, PACK], F32, name="squashed")
         for h in range(J // P):
             cols = slice(h * P, (h + 1) * P)
             raw = ps.tile([P, PACK, P], F32, name=f"raw{h}")
@@ -123,15 +123,12 @@ def tile_attend_tab_plain_merge_kernel(tc, keys_words, keys_scales, notes, rowf,
                     start=True,
                     stop=True,
                 )
-            squashed = sb.tile([P, P, PACK], F32, name=f"squashed{h}", tag=f"squashed{h}", align_bytes=64)
-            nc.scalar.activation(squashed[:], raw[:].rearrange("p t j -> p j t"), ACT.Tanh)
-            table_bf = table_both[:, h]
-            nc.vector.tensor_tensor(
-                table_bf, squashed[:], row_factor[:].unsqueeze(1).to_broadcast([P, P, PACK]), ALU.mult
-            )
-            nc.vector.quantize_mx(
-                table_words[:, cols].bitcast(FP8X4), table_bytes[:, cols], table_bf.rearrange("p j t -> p (j t)")
-            )
+            nc.scalar.activation(squashed[:, cols, :], raw[:].rearrange("p t j -> p j t"), ACT.Tanh)
+        table_bf = sb.tile([P, J, PACK], BF16, name="table_bf", tag="vals0", align_bytes=64)
+        nc.vector.tensor_tensor(
+            table_bf[:], squashed[:], row_factor[:].unsqueeze(1).to_broadcast([P, J, PACK]), ALU.mult
+        )
+        nc.vector.quantize_mx(table_words[:].bitcast(FP8X4), table_bytes[:], table_bf[:].rearrange("p j t -> p (j t)"))
 
         last = PACK - 1
 
@@ -143,8 +140,8 @@ def tile_attend_tab_plain_merge_kernel(tc, keys_words, keys_scales, notes, rowf,
             copy(val_bf.bitcast(F32), turned[:].rearrange("p u c -> p c u"))
 
         def multiply(val_bf, blocks):
-            val_words = sb.tile([P, blocks * P], U32, name="val_words", bufs=4, align_bytes=64)
-            val_bytes = sb.tile([P, blocks * P], U8, name="val_bytes", bufs=4, align_bytes=64)
+            val_words = sb.tile([P, blocks * P], U32, name="val_words", bufs=3, align_bytes=64)
+            val_bytes = sb.tile([P, blocks * P], U8, name="val_bytes", bufs=3, align_bytes=64)
             nc.vector.quantize_mx(val_words[:].bitcast(FP8X4), val_bytes[:], val_bf)
             summed = ps2.tile([P, blocks, J], F32, name="summed")
             for k in range(blocks):
@@ -159,20 +156,14 @@ def tile_attend_tab_plain_merge_kernel(tc, keys_words, keys_scales, notes, rowf,
                 )
             return summed
 
-        gained = []
-        for b in range(2):
-            picked = sb.tile([P, I], BF16, name=f"picked{b}", tag=("keys", "squashed0")[b], align_bytes=64)
-            if b == 0:
-                nc.vector.tensor_copy(picked[:], val_pool[b][:].indirect(idx[:]))
-                val_bf = sb.tile([P, P, PACK], BF16, name="val_bf0", align_bytes=64)
-            else:
-                nc.scalar.activation(picked[:], val_pool[b][:].indirect(idx[:]), ACT.Copy)
-                val_bf = both.tile([P, P, PACK], BF16, name="val_bf1", offset=8192, align_bytes=64)
-            turn(picked, val_bf[:], nc.vector.tensor_copy)
-            summed = multiply(val_bf[:].rearrange("p c t -> p (c t)"), 1)
-            scaled = sb.tile([P, J], F32, name=f"gained{b}")
-            nc.vector.tensor_tensor(scaled[:], summed[:, 0, :], gain[:], ALU.mult)
-            gained.append(scaled)
+        val_bf01 = both.tile([P, 2, P, PACK], BF16, name="val_bf01", offset=8192, align_bytes=64)
+        picked0 = sb.tile([P, I], BF16, name="picked0", tag="keys", align_bytes=64)
+        nc.vector.tensor_copy(picked0[:], val_pool[0][:].indirect(idx[:]))
+        turn(picked0, val_bf01[:, 0], nc.vector.tensor_copy)
+        picked1 = sb.tile([P, I], BF16, name="picked1", tag="note_words", align_bytes=64)
+        nc.scalar.activation(picked1[:], val_pool[1][:].indirect(idx[:]), ACT.Copy)
+        turn(picked1, val_bf01[:, 1], nc.vector.tensor_copy)
+        summed01 = multiply(val_bf01[:].rearrange("p k c t -> p (k c t)"), 2)
 
         picked2 = sb.tile([P, I], BF16, name="picked2", tag="vals1", align_bytes=64)
         nc.scalar.activation(picked2[:], val_pool[2][:].indirect(idx[:]), ACT.Copy)
@@ -180,7 +171,9 @@ def tile_attend_tab_plain_merge_kernel(tc, keys_words, keys_scales, notes, rowf,
         split = 320
         nc.vector.tensor_copy(picked3[:, :split], val_pool[last][:].indirect(idx[:, : split // 16]))
         nc.scalar.activation(picked3[:, split:], val_pool[last][:].indirect(idx[:, split // 16 :]), ACT.Copy)
-        val_bf2 = both.tile([P, P, PACK], BF16, name="val_bf2", offset=9216, align_bytes=64)
+        gained01 = both.tile([P, 2, J], F32, name="gained01", offset=10240 + 4096, align_bytes=64)
+        nc.vector.tensor_tensor(gained01[:], summed01[:], gain[:].unsqueeze(1).to_broadcast([P, 2, J]), ALU.mult)
+        val_bf2 = both.tile([P, P, PACK], BF16, name="val_bf2", offset=10240, align_bytes=64)
         turn(picked2, val_bf2[:], nc.scalar.copy)
         summed2 = multiply(val_bf2[:].rearrange("p c t -> p (c t)"), 1)
         val_bf3 = sb.tile([P, P, PACK], BF16, name="val_bf3", tag="val_bf3", align_bytes=64)
@@ -188,7 +181,7 @@ def tile_attend_tab_plain_merge_kernel(tc, keys_words, keys_scales, notes, rowf,
         summed3 = multiply(val_bf3[:].rearrange("p c t -> p (c t)"), 1)
 
         looked = [
-            both.tile([P, J], F32, name="looked0", offset=9216 + 2048, align_bytes=64),
+            both.tile([P, J], F32, name="looked0", offset=10240 + 2048, align_bytes=64),
             sb.tile([P, J], F32, name="looked1", tag="held0", align_bytes=64),
             sb.tile([P, J], F32, name="looked2", tag="held1", align_bytes=64),
         ]
@@ -199,7 +192,7 @@ def tile_attend_tab_plain_merge_kernel(tc, keys_words, keys_scales, notes, rowf,
         gained3 = sb.tile([P, J], F32, name="gained3")
         nc.vector.tensor_tensor(gained3[:], summed3[:, 0, :], gain[:], ALU.mult)
         for b in range(2):
-            nc.vector.tensor_tensor(first[:, b, :], looked[b][:], gained[b][:], ALU.add)
+            nc.vector.tensor_tensor(first[:, b, :], looked[b][:], gained01[:, b, :], ALU.add)
         nc.sync.dma_start(out_v[:, 0:2, :], first[:, 0:2, :])
         third = sb.tile([P, J], F32, name="third", tag="gain", align_bytes=64)
         nc.vector.tensor_tensor(third[:], looked[2][:], first[:, 2, :], ALU.add)

@@ -18,104 +18,122 @@ ACT = mybir.ActivationFunctionType
 ALU = mybir.AluOpType
 
 P = 128
-PACK = 4
+PLACES = 4
+BLOCKS = E // P
+HALVES = J // P
+QUADRANTS = 4
+PER_COLUMN = 16
+ALIGN = 64
+
+LAST_VALUES_ON_VECTOR = 320
+MERGE2_ON_VECTOR = 96
+
+VALS2_AT = 0
+TURNED01_AT = VALS2_AT + 4 * T
+VALS3_AT = TURNED01_AT + 2 * (2 * I)
+PICKED3_AT = TURNED01_AT - I
+TURNED2_AT = VALS3_AT
+LOOKED0_AT = VALS3_AT + 2048
+GAINED01_AT = VALS3_AT + 4096
 
 
-def tile_attend_tab_plain_merge_kernel(tc, keys_words, keys_scales, notes, rowf, vals, held, hgain, offs, offs2, offs3, out):
+def tile_attend_tab_plain_merge_kernel(
+    tc, keys_words, keys_scales, notes, rowf, vals, held, hgain, offs, offs2, offs3, out
+):
     nc = tc.nc
     with ExitStack() as ctx:
         sb = ctx.enter_context(tc.tile_pool(name="sb", bufs=1))
-        both = ctx.enter_context(tc.tile_pool(name="both", bufs=1))
+        shared = ctx.enter_context(tc.tile_pool(name="shared", bufs=1))
         ps = ctx.enter_context(tc.psum_pool(name="ps", bufs=1))
         ps2 = ctx.enter_context(tc.psum_pool(name="ps2", bufs=2))
 
-        idx = sb.tile([P, I // 16], U16, name="idx")
-        idx2 = sb.tile([P, J // 16], U16, name="idx2")
-        idx3 = sb.tile([P, J // 16], U16, name="idx3")
-        key_pool = sb.tile([P, T], U32, name="key_pool", tag="keys", align_bytes=64)
-        scale_pool = sb.tile([P, T], U8, name="scale_pool")
-        gain_pool = sb.tile([P, M], F32, name="gain_pool")
-        row_factor = sb.tile([P, PACK], F32, name="row_factor")
-        note_pool = [sb.tile([P, 2, U], F32, name=f"note_pool{a}", tag=f"notes{a}", align_bytes=64) for a in range(2)]
-        val_pool = [
-            both.tile([P, T], F32, name=f"val_pool{b}", offset=(0, 10240)[b - 2], align_bytes=64)
-            if b >= 2
-            else sb.tile([P, T], F32, name=f"val_pool{b}", tag=f"vals{b}", align_bytes=64)
-            for b in range(PACK)
+        idx = sb.tile([P, I // PER_COLUMN], U16, name="idx")
+        idx2 = sb.tile([P, J // PER_COLUMN], U16, name="idx2")
+        idx3 = sb.tile([P, J // PER_COLUMN], U16, name="idx3")
+        key_table = sb.tile([P, T], U32, name="key_table", tag="keys", align_bytes=ALIGN)
+        scale_table = sb.tile([P, T], U8, name="scale_table")
+        gain_table = sb.tile([P, M], F32, name="gain_table")
+        row_factor = sb.tile([P, PLACES], F32, name="row_factor")
+        note_tables = [sb.tile([P, 2, U], F32, name=f"note_table{a}", tag=f"notes{a}", align_bytes=ALIGN) for a in range(2)]
+        val_tables = [
+            sb.tile([P, T], F32, name="val_table0", tag="vals0", align_bytes=ALIGN),
+            sb.tile([P, T], F32, name="val_table1", tag="vals1", align_bytes=ALIGN),
+            shared.tile([P, T], F32, name="val_table2", offset=VALS2_AT, align_bytes=ALIGN),
+            shared.tile([P, T], F32, name="val_table3", offset=VALS3_AT, align_bytes=ALIGN),
         ]
-        held_pool = [sb.tile([P, M], F32, name=f"held_pool{b}", tag=f"held{b}", align_bytes=64) for b in range(PACK)]
+        held_tables = [sb.tile([P, M], F32, name=f"held_table{b}", tag=f"held{b}", align_bytes=ALIGN) for b in range(BLOCKS)]
         ident = sb.tile([P, P], F32, name="ident")
 
         scale_rows = sb.tile([P, T // 4], I32, name="scale_rows")
-        gain_first = sb.tile([1, M], F32, name="gain_first")
-        nc.vector.memset(scale_pool[:].bitcast(I32), 0)
-        nc.gpsimd.memset(gain_pool[:], 0.0)
+        gain_row = sb.tile([1, M], F32, name="gain_row")
+        nc.vector.memset(scale_table[:].bitcast(I32), 0)
+        nc.gpsimd.memset(gain_table[:], 0.0)
         make_identity(nc, ident[:])
 
-        notes_v = notes.rearrange("(p t) u -> p t u", t=PACK)
-        vals_v = vals.rearrange("(p b) t -> p b t", b=PACK)
-        held_v = held.rearrange("(p b) m -> p b m", b=PACK)
-        out_v = out.rearrange("(p b) j -> p b j", b=PACK)
+        notes_by_place = notes.rearrange("(p t) u -> p t u", t=PLACES)
+        vals_by_block = vals.rearrange("(p b) t -> p b t", b=BLOCKS)
+        held_by_block = held.rearrange("(p b) m -> p b m", b=BLOCKS)
+        out_by_block = out.rearrange("(p b) j -> p b j", b=BLOCKS)
 
         nc.sync.dma_start(idx2[:], offs2)
         nc.sync.dma_start(idx[:], offs)
         for a in range(2):
-            nc.sync.dma_start(note_pool[a][:], notes_v[:, 2 * a : 2 * a + 2, :])
+            nc.sync.dma_start(note_tables[a][:], notes_by_place[:, 2 * a : 2 * a + 2, :])
         nc.sync.dma_start(idx3[:], offs3)
-        nc.sync.dma_start(key_pool[:].bitcast(I32), keys_words[0].rearrange("p n r -> p (n r)").bitcast(I32))
-        for b in range(PACK):
-            nc.sync.dma_start(val_pool[b][:], vals_v[:, b, :])
-        for b in range(PACK):
-            nc.sync.dma_start(held_pool[b][:], held_v[:, b, :])
-        for q in range(4):
-            nc.scalar.dma_start(scale_rows[32 * q : 32 * q + 4, :], keys_scales[0, 4 * q : 4 * q + 4, :].bitcast(I32))
-        nc.scalar.dma_start(gain_first[:], hgain[0:1, :])
-        nc.scalar.dma_start(row_factor[:], rowf.rearrange("(p t) o -> p (t o)", t=PACK))
+        nc.sync.dma_start(key_table[:].bitcast(I32), keys_words[0].rearrange("p n r -> p (n r)").bitcast(I32))
+        for b in range(BLOCKS):
+            nc.sync.dma_start(val_tables[b][:], vals_by_block[:, b, :])
+        for b in range(BLOCKS):
+            nc.sync.dma_start(held_tables[b][:], held_by_block[:, b, :])
+        for g in range(QUADRANTS):
+            nc.scalar.dma_start(scale_rows[32 * g : 32 * g + 4, :], keys_scales[0, 4 * g : 4 * g + 4, :].bitcast(I32))
+        nc.scalar.dma_start(gain_row[:], hgain[0:1, :])
+        nc.scalar.dma_start(row_factor[:], rowf.rearrange("(p t) o -> p (t o)", t=PLACES))
 
-        for q in range(4):
-            nc.vector.tensor_copy(scale_pool[32 * q : 32 * q + 4, :].bitcast(I32), scale_rows[32 * q : 32 * q + 4, :])
-        nc.scalar.activation(gain_pool[0:1, :], gain_first[:], ACT.Copy)
+        for g in range(QUADRANTS):
+            nc.vector.tensor_copy(scale_table[32 * g : 32 * g + 4, :].bitcast(I32), scale_rows[32 * g : 32 * g + 4, :])
+        nc.scalar.activation(gain_table[0:1, :], gain_row[:], ACT.Copy)
 
-        key_bytes = sb.tile([P, I], U8, name="key_bytes", align_bytes=64)
-        nc.vector.tensor_copy(key_bytes[:].rearrange("p (t s) -> p s t", t=PACK), scale_pool[:].indirect(idx[:]))
+        key_bytes = sb.tile([P, I], U8, name="key_bytes", align_bytes=ALIGN)
+        nc.vector.tensor_copy(key_bytes[:].rearrange("p (t s) -> p s t", t=PLACES), scale_table[:].indirect(idx[:]))
 
         note_planes = sb.tile([P, 2, J], F32, name="note_planes")
-        note_bf = sb.tile([P, J, PACK], BF16, name="note_bf", align_bytes=64)
-        for t in range(2):
-            nc.scalar.activation(note_planes[:, t, :], note_pool[0][:, t, :].indirect(idx2[:]), ACT.Copy)
-        nc.scalar.activation(note_bf[:, :, 0:2], note_planes[:].rearrange("p t j -> p j t"), ACT.Copy)
-        for t in range(2):
-            nc.vector.tensor_copy(note_bf[:, :, 2 + t], note_pool[1][:, t, :].indirect(idx2[:]))
-        note_words = sb.tile([P, J], U32, name="note_words", tag="note_words", align_bytes=64)
-        note_bytes = sb.tile([P, J], U8, name="note_bytes", align_bytes=64)
+        note_bf = sb.tile([P, J, PLACES], BF16, name="note_bf", align_bytes=ALIGN)
+        for s in range(2):
+            nc.scalar.activation(note_planes[:, s, :], note_tables[0][:, s, :].indirect(idx2[:]), ACT.Copy)
+        nc.scalar.activation(note_bf[:, :, 0:2], note_planes[:].rearrange("p s j -> p j s"), ACT.Copy)
+        for s in range(2):
+            nc.vector.tensor_copy(note_bf[:, :, 2 + s], note_tables[1][:, s, :].indirect(idx2[:]))
+        note_words = sb.tile([P, J], U32, name="note_words", tag="note_words", align_bytes=ALIGN)
+        note_bytes = sb.tile([P, J], U8, name="note_bytes", align_bytes=ALIGN)
         nc.vector.quantize_mx(note_words[:].bitcast(FP8X4), note_bytes[:], note_bf[:].rearrange("p j t -> p (j t)"))
 
-        key_words = sb.tile([P, I], U32, name="key_words", tag="notes1", align_bytes=64)
-        nc.vector.tensor_copy(key_words[:].rearrange("p (t s) -> p s t", t=PACK), key_pool[:].indirect(idx[:]))
+        key_words = sb.tile([P, I], U32, name="key_words", tag="notes1", align_bytes=ALIGN)
+        nc.vector.tensor_copy(key_words[:].rearrange("p (t s) -> p s t", t=PLACES), key_table[:].indirect(idx[:]))
 
-        gain_row = sb.tile([P, J], F32, name="gain_row")
-        nc.scalar.activation(gain_row[:], gain_pool[:].indirect(idx3[:]), ACT.Copy)
-        gain_turned = ps.tile([P, J // P, P], F32, name="gain_turned")
-        for h in range(J // P):
-            nc.tensor.transpose(gain_turned[:, h, :], gain_row[:, h * P : (h + 1) * P], ident[:])
-        gain_col = sb.tile([P, J // P], F32, name="gain_col")
-        nc.scalar.copy(gain_col[:], gain_turned[:, :, 0])
-        gain_spread = ps.tile([P, J // P, P], F32, name="gain_spread")
-        for h in range(J // P):
-            nc.tensor.transpose(gain_spread[:, h, :], gain_col[:, h : h + 1].to_broadcast([P, P]), ident[:])
-        gain = sb.tile([P, J], F32, name="gain", tag="gain", align_bytes=64)
+        gain_picked = sb.tile([P, J], F32, name="gain_picked")
+        nc.scalar.activation(gain_picked[:], gain_table[:].indirect(idx3[:]), ACT.Copy)
+        gain_turned = ps.tile([P, HALVES, P], F32, name="gain_turned")
+        for h in range(HALVES):
+            nc.tensor.transpose(gain_turned[:, h, :], gain_picked[:, h * P : (h + 1) * P], ident[:])
+        gain_column = sb.tile([P, HALVES], F32, name="gain_column")
+        nc.scalar.copy(gain_column[:], gain_turned[:, :, 0])
+        gain_spread = ps.tile([P, HALVES, P], F32, name="gain_spread")
+        for h in range(HALVES):
+            nc.tensor.transpose(gain_spread[:, h, :], gain_column[:, h : h + 1].to_broadcast([P, P]), ident[:])
+        gain = sb.tile([P, J], F32, name="gain", tag="gain", align_bytes=ALIGN)
         nc.scalar.copy(gain[:], gain_spread[:].rearrange("p h j -> p (h j)"))
 
-        table_words = sb.tile([P, J], U32, name="table_words", align_bytes=64)
-        table_bytes = sb.tile([P, J], U8, name="table_bytes", align_bytes=64)
-        squashed = sb.tile([P, J, PACK], F32, name="squashed")
-        for h in range(J // P):
+        gr1_words = sb.tile([P, J], U32, name="gr1_words", align_bytes=ALIGN)
+        gr1_bytes = sb.tile([P, J], U8, name="gr1_bytes", align_bytes=ALIGN)
+        g0 = sb.tile([P, J, PLACES], F32, name="g0")
+        for h in range(HALVES):
             cols = slice(h * P, (h + 1) * P)
-            raw = ps.tile([P, PACK, P], F32, name=f"raw{h}")
-            for t in range(PACK):
+            g9 = ps.tile([P, PLACES, P], F32, name=f"g9_half{h}")
+            for t in range(PLACES):
                 rows = slice(t * P, (t + 1) * P)
                 nc.tensor.matmul_mx(
-                    raw[:, t, :],
+                    g9[:, t, :],
                     lhsT=key_words[:, rows].bitcast(FP8X4),
                     lhsT_scale=key_bytes[:, rows],
                     rhs=note_words[:, cols].bitcast(FP8X4),
@@ -123,80 +141,83 @@ def tile_attend_tab_plain_merge_kernel(tc, keys_words, keys_scales, notes, rowf,
                     start=True,
                     stop=True,
                 )
-            nc.scalar.activation(squashed[:, cols, :], raw[:].rearrange("p t j -> p j t"), ACT.Tanh)
-        table_bf = sb.tile([P, J, PACK], BF16, name="table_bf", tag="vals0", align_bytes=64)
-        nc.vector.tensor_tensor(
-            table_bf[:], squashed[:], row_factor[:].unsqueeze(1).to_broadcast([P, J, PACK]), ALU.mult
-        )
-        nc.vector.quantize_mx(table_words[:].bitcast(FP8X4), table_bytes[:], table_bf[:].rearrange("p j t -> p (j t)"))
+            nc.scalar.activation(g0[:, cols, :], g9[:].rearrange("p t j -> p j t"), ACT.Tanh)
+        gr1_bf = sb.tile([P, J, PLACES], BF16, name="gr1_bf", tag="vals0", align_bytes=ALIGN)
+        nc.vector.tensor_tensor(gr1_bf[:], g0[:], row_factor[:].unsqueeze(1).to_broadcast([P, J, PLACES]), ALU.mult)
+        nc.vector.quantize_mx(gr1_words[:].bitcast(FP8X4), gr1_bytes[:], gr1_bf[:].rearrange("p j t -> p (j t)"))
 
-        last = PACK - 1
-
-        def turn(picked, val_bf, copy):
+        def turn(picked, turned, copy):
             pairs = picked[:].bitcast(F32)
-            turned = ps2.tile([P, 2, P], F32, name="turned")
+            bank = ps2.tile([P, 2, P], F32, name="turn_bank")
             for u in range(2):
-                nc.tensor.transpose(turned[:, u, :], pairs[:, u : I // 2 : 2], ident[:])
-            copy(val_bf.bitcast(F32), turned[:].rearrange("p u c -> p c u"))
+                nc.tensor.transpose(bank[:, u, :], pairs[:, u : I // 2 : 2], ident[:])
+            copy(turned.bitcast(F32), bank[:].rearrange("p u c -> p c u"))
 
-        def multiply(val_bf, blocks):
-            val_words = sb.tile([P, blocks * P], U32, name="val_words", bufs=3, align_bytes=64)
-            val_bytes = sb.tile([P, blocks * P], U8, name="val_bytes", bufs=3, align_bytes=64)
-            nc.vector.quantize_mx(val_words[:].bitcast(FP8X4), val_bytes[:], val_bf)
-            summed = ps2.tile([P, blocks, J], F32, name="summed")
-            for k in range(blocks):
+        def multiply(turned, count):
+            val_words = sb.tile([P, count * P], U32, name="val_words", bufs=3, align_bytes=ALIGN)
+            val_bytes = sb.tile([P, count * P], U8, name="val_bytes", bufs=3, align_bytes=ALIGN)
+            nc.vector.quantize_mx(val_words[:].bitcast(FP8X4), val_bytes[:], turned)
+            sums = ps2.tile([P, count, J], F32, name="sums")
+            for n in range(count):
                 nc.tensor.matmul_mx(
-                    summed[:, k, :],
-                    lhsT=val_words[:, k * P : (k + 1) * P].bitcast(FP8X4),
-                    lhsT_scale=val_bytes[:, k * P : (k + 1) * P],
-                    rhs=table_words[:].bitcast(FP8X4),
-                    rhs_scale=table_bytes[:],
+                    sums[:, n, :],
+                    lhsT=val_words[:, n * P : (n + 1) * P].bitcast(FP8X4),
+                    lhsT_scale=val_bytes[:, n * P : (n + 1) * P],
+                    rhs=gr1_words[:].bitcast(FP8X4),
+                    rhs_scale=gr1_bytes[:],
                     start=True,
                     stop=True,
                 )
-            return summed
+            return sums
 
-        val_bf01 = both.tile([P, 2, P, PACK], BF16, name="val_bf01", offset=8192, align_bytes=64)
-        picked0 = sb.tile([P, I], BF16, name="picked0", tag="keys", align_bytes=64)
-        nc.vector.tensor_copy(picked0[:], val_pool[0][:].indirect(idx[:]))
-        turn(picked0, val_bf01[:, 0], nc.vector.tensor_copy)
-        picked1 = sb.tile([P, I], BF16, name="picked1", tag="note_words", align_bytes=64)
-        nc.scalar.activation(picked1[:], val_pool[1][:].indirect(idx[:]), ACT.Copy)
-        turn(picked1, val_bf01[:, 1], nc.vector.tensor_copy)
-        summed01 = multiply(val_bf01[:].rearrange("p k c t -> p (k c t)"), 2)
+        turned01 = shared.tile([P, 2, P, PLACES], BF16, name="turned01", offset=TURNED01_AT, align_bytes=ALIGN)
+        picked0 = sb.tile([P, I], BF16, name="picked0", tag="keys", align_bytes=ALIGN)
+        nc.vector.tensor_copy(picked0[:], val_tables[0][:].indirect(idx[:]))
+        turn(picked0, turned01[:, 0], nc.vector.tensor_copy)
+        picked1 = sb.tile([P, I], BF16, name="picked1", tag="note_words", align_bytes=ALIGN)
+        nc.scalar.activation(picked1[:], val_tables[1][:].indirect(idx[:]), ACT.Copy)
+        turn(picked1, turned01[:, 1], nc.vector.tensor_copy)
+        sums01 = multiply(turned01[:].rearrange("p n c t -> p (n c t)"), 2)
 
-        picked2 = sb.tile([P, I], BF16, name="picked2", tag="vals1", align_bytes=64)
-        nc.scalar.activation(picked2[:], val_pool[2][:].indirect(idx[:]), ACT.Copy)
-        picked3 = both.tile([P, I], BF16, name="picked3", offset=8192 - I, align_bytes=64)
-        split = 320
-        nc.vector.tensor_copy(picked3[:, :split], val_pool[last][:].indirect(idx[:, : split // 16]))
-        nc.scalar.activation(picked3[:, split:], val_pool[last][:].indirect(idx[:, split // 16 :]), ACT.Copy)
-        gained01 = both.tile([P, 2, J], F32, name="gained01", offset=10240 + 4096, align_bytes=64)
-        nc.vector.tensor_tensor(gained01[:], summed01[:], gain[:].unsqueeze(1).to_broadcast([P, 2, J]), ALU.mult)
-        val_bf2 = both.tile([P, P, PACK], BF16, name="val_bf2", offset=10240, align_bytes=64)
-        turn(picked2, val_bf2[:], nc.scalar.copy)
-        summed2 = multiply(val_bf2[:].rearrange("p c t -> p (c t)"), 1)
-        val_bf3 = sb.tile([P, P, PACK], BF16, name="val_bf3", tag="val_bf3", align_bytes=64)
-        turn(picked3, val_bf3[:], nc.vector.tensor_copy)
-        summed3 = multiply(val_bf3[:].rearrange("p c t -> p (c t)"), 1)
+        picked2 = sb.tile([P, I], BF16, name="picked2", tag="vals1", align_bytes=ALIGN)
+        nc.scalar.activation(picked2[:], val_tables[2][:].indirect(idx[:]), ACT.Copy)
+        picked3 = shared.tile([P, I], BF16, name="picked3", offset=PICKED3_AT, align_bytes=ALIGN)
+        cut = LAST_VALUES_ON_VECTOR
+        nc.vector.tensor_copy(picked3[:, :cut], val_tables[3][:].indirect(idx[:, : cut // PER_COLUMN]))
+        nc.scalar.activation(picked3[:, cut:], val_tables[3][:].indirect(idx[:, cut // PER_COLUMN :]), ACT.Copy)
+        gained01 = shared.tile([P, 2, J], F32, name="gained01", offset=GAINED01_AT, align_bytes=ALIGN)
+        nc.vector.tensor_tensor(gained01[:], sums01[:], gain[:].unsqueeze(1).to_broadcast([P, 2, J]), ALU.mult)
+        turned2 = shared.tile([P, P, PLACES], BF16, name="turned2", offset=TURNED2_AT, align_bytes=ALIGN)
+        turn(picked2, turned2[:], nc.scalar.copy)
+        sums2 = multiply(turned2[:].rearrange("p c t -> p (c t)"), 1)
+        turned3 = sb.tile([P, P, PLACES], BF16, name="turned3", tag="turned3", align_bytes=ALIGN)
+        turn(picked3, turned3[:], nc.vector.tensor_copy)
+        sums3 = multiply(turned3[:].rearrange("p c t -> p (c t)"), 1)
 
         looked = [
-            both.tile([P, J], F32, name="looked0", offset=10240 + 2048, align_bytes=64),
-            sb.tile([P, J], F32, name="looked1", tag="held0", align_bytes=64),
-            sb.tile([P, J], F32, name="looked2", tag="held1", align_bytes=64),
+            shared.tile([P, J], F32, name="looked0", offset=LOOKED0_AT, align_bytes=ALIGN),
+            sb.tile([P, J], F32, name="looked1", tag="held0", align_bytes=ALIGN),
+            sb.tile([P, J - MERGE2_ON_VECTOR], F32, name="looked2", tag="held1", align_bytes=ALIGN),
         ]
-        for b in range(last):
-            nc.scalar.activation(looked[b][:], held_pool[b][:].indirect(idx3[:]), ACT.Copy)
-        first = sb.tile([P, 3, J], F32, name="first", tag="val_bf3", align_bytes=64)
-        nc.vector.tensor_tensor(first[:, 2, :], summed2[:, 0, :], gain[:], ALU.mult)
-        gained3 = sb.tile([P, J], F32, name="gained3")
-        nc.vector.tensor_tensor(gained3[:], summed3[:, 0, :], gain[:], ALU.mult)
         for b in range(2):
-            nc.vector.tensor_tensor(first[:, b, :], looked[b][:], gained01[:, b, :], ALU.add)
-        nc.sync.dma_start(out_v[:, 0:2, :], first[:, 0:2, :])
-        third = sb.tile([P, J], F32, name="third", tag="gain", align_bytes=64)
-        nc.vector.tensor_tensor(third[:], looked[2][:], first[:, 2, :], ALU.add)
-        nc.sync.dma_start(out_v[:, 2, :], third[:])
-        fourth = sb.tile([P, J], F32, name="fourth", tag="held1", align_bytes=64)
-        nc.vector.tensor_tensor(fourth[:], held_pool[last][:].indirect(idx3[:]), gained3[:], ALU.add)
-        nc.sync.dma_start(out_v[:, last, :], fourth[:])
+            nc.scalar.activation(looked[b][:], held_tables[b][:].indirect(idx3[:]), ACT.Copy)
+        split = MERGE2_ON_VECTOR
+        nc.scalar.activation(looked[2][:], held_tables[2][:].indirect(idx3[:, split // PER_COLUMN :]), ACT.Copy)
+        after_last_quantise = sb.tile([P, 3, J], F32, name="after_last_quantise", tag="turned3", align_bytes=ALIGN)
+        result01 = after_last_quantise[:, 0:2, :]
+        gained2 = after_last_quantise[:, 2, :]
+        nc.vector.tensor_tensor(gained2, sums2[:, 0, :], gain[:], ALU.mult)
+        gained3 = sb.tile([P, J], F32, name="gained3")
+        nc.vector.tensor_tensor(gained3[:], sums3[:, 0, :], gain[:], ALU.mult)
+        for b in range(2):
+            nc.vector.tensor_tensor(result01[:, b, :], looked[b][:], gained01[:, b, :], ALU.add)
+        nc.sync.dma_start(out_by_block[:, 0:2, :], result01)
+        result2 = sb.tile([P, J], F32, name="result2", tag="gain", align_bytes=ALIGN)
+        nc.vector.tensor_tensor(
+            result2[:, :split], held_tables[2][:].indirect(idx3[:, : split // PER_COLUMN]), gained2[:, :split], ALU.add
+        )
+        nc.vector.tensor_tensor(result2[:, split:], looked[2][:], gained2[:, split:], ALU.add)
+        nc.sync.dma_start(out_by_block[:, 2, :], result2[:])
+        result3 = sb.tile([P, J], F32, name="result3", tag="held1", align_bytes=ALIGN)
+        nc.vector.tensor_tensor(result3[:], held_tables[3][:].indirect(idx3[:]), gained3[:], ALU.add)
+        nc.sync.dma_start(out_by_block[:, 3, :], result3[:])

from contextlib import ExitStack

import concourse.mybir as mybir
from concourse.masks import make_identity

D, T, I, J, U, E, M = 512, 2048, 512, 256, 1024, 512, 1024
FLOPS = 2 * D * I * J + 2 * I * E * J
BYTES = D * T + 16 * T + 4 * (D * U + I + E * T + E * M + M + E * J) + 2 * 128 * (I + J + J) // 16

F32 = mybir.dt.float32
BF16 = mybir.dt.bfloat16
I32 = mybir.dt.int32
U32 = mybir.dt.uint32
U16 = mybir.dt.uint16
U8 = mybir.dt.uint8
FP8X4 = mybir.dt.float8_e4m3fn_x4
ACT = mybir.ActivationFunctionType
ALU = mybir.AluOpType

P = 128
PLACES = 4
BLOCKS = E // P
HALVES = J // P
QUADRANTS = 4
PER_COLUMN = 16
ALIGN = 64

LAST_VALUES_ON_VECTOR = 320
MERGE2_ON_VECTOR = 96

VALS2_AT = 0
TURNED01_AT = VALS2_AT + 4 * T
VALS3_AT = TURNED01_AT + 2 * (2 * I)
PICKED3_AT = TURNED01_AT - I
TURNED2_AT = VALS3_AT
LOOKED0_AT = VALS3_AT + 2048
GAINED01_AT = VALS3_AT + 4096


def tile_attend_tab_plain_merge_kernel(
    tc, keys_words, keys_scales, notes, rowf, vals, held, hgain, offs, offs2, offs3, out
):
    nc = tc.nc
    with ExitStack() as ctx:
        sb = ctx.enter_context(tc.tile_pool(name="sb", bufs=1))
        shared = ctx.enter_context(tc.tile_pool(name="shared", bufs=1))
        ps = ctx.enter_context(tc.psum_pool(name="ps", bufs=1))
        ps2 = ctx.enter_context(tc.psum_pool(name="ps2", bufs=2))

        idx = sb.tile([P, I // PER_COLUMN], U16, name="idx")
        idx2 = sb.tile([P, J // PER_COLUMN], U16, name="idx2")
        idx3 = sb.tile([P, J // PER_COLUMN], U16, name="idx3")
        key_table = sb.tile([P, T], U32, name="key_table", tag="keys", align_bytes=ALIGN)
        scale_table = sb.tile([P, T], U8, name="scale_table")
        gain_table = sb.tile([P, M], F32, name="gain_table")
        row_factor = sb.tile([P, PLACES], F32, name="row_factor")
        note_tables = [sb.tile([P, 2, U], F32, name=f"note_table{a}", tag=f"notes{a}", align_bytes=ALIGN) for a in range(2)]
        val_tables = [
            sb.tile([P, T], F32, name="val_table0", tag="vals0", align_bytes=ALIGN),
            sb.tile([P, T], F32, name="val_table1", tag="vals1", align_bytes=ALIGN),
            shared.tile([P, T], F32, name="val_table2", offset=VALS2_AT, align_bytes=ALIGN),
            shared.tile([P, T], F32, name="val_table3", offset=VALS3_AT, align_bytes=ALIGN),
        ]
        held_tables = [sb.tile([P, M], F32, name=f"held_table{b}", tag=f"held{b}", align_bytes=ALIGN) for b in range(BLOCKS)]
        ident = sb.tile([P, P], F32, name="ident")

        scale_rows = sb.tile([P, T // 4], I32, name="scale_rows")
        gain_row = sb.tile([1, M], F32, name="gain_row")
        nc.vector.memset(scale_table[:].bitcast(I32), 0)
        nc.gpsimd.memset(gain_table[:], 0.0)
        make_identity(nc, ident[:])

        notes_by_place = notes.rearrange("(p t) u -> p t u", t=PLACES)
        vals_by_block = vals.rearrange("(p b) t -> p b t", b=BLOCKS)
        held_by_block = held.rearrange("(p b) m -> p b m", b=BLOCKS)
        out_by_block = out.rearrange("(p b) j -> p b j", b=BLOCKS)

        nc.sync.dma_start(idx2[:], offs2)
        nc.sync.dma_start(idx[:], offs)
        for a in range(2):
            nc.sync.dma_start(note_tables[a][:], notes_by_place[:, 2 * a : 2 * a + 2, :])
        nc.sync.dma_start(idx3[:], offs3)
        nc.sync.dma_start(key_table[:].bitcast(I32), keys_words[0].rearrange("p n r -> p (n r)").bitcast(I32))
        for b in range(BLOCKS):
            nc.sync.dma_start(val_tables[b][:], vals_by_block[:, b, :])
        for b in range(BLOCKS):
            nc.sync.dma_start(held_tables[b][:], held_by_block[:, b, :])
        for g in range(QUADRANTS):
            nc.scalar.dma_start(scale_rows[32 * g : 32 * g + 4, :], keys_scales[0, 4 * g : 4 * g + 4, :].bitcast(I32))
        nc.scalar.dma_start(gain_row[:], hgain[0:1, :])
        nc.scalar.dma_start(row_factor[:], rowf.rearrange("(p t) o -> p (t o)", t=PLACES))

        for g in range(QUADRANTS):
            nc.vector.tensor_copy(scale_table[32 * g : 32 * g + 4, :].bitcast(I32), scale_rows[32 * g : 32 * g + 4, :])
        nc.scalar.activation(gain_table[0:1, :], gain_row[:], ACT.Copy)

        key_bytes = sb.tile([P, I], U8, name="key_bytes", align_bytes=ALIGN)
        nc.vector.tensor_copy(key_bytes[:].rearrange("p (t s) -> p s t", t=PLACES), scale_table[:].indirect(idx[:]))

        note_planes = sb.tile([P, 2, J], F32, name="note_planes")
        note_bf = sb.tile([P, J, PLACES], BF16, name="note_bf", align_bytes=ALIGN)
        for s in range(2):
            nc.scalar.activation(note_planes[:, s, :], note_tables[0][:, s, :].indirect(idx2[:]), ACT.Copy)
        nc.scalar.activation(note_bf[:, :, 0:2], note_planes[:].rearrange("p s j -> p j s"), ACT.Copy)
        for s in range(2):
            nc.vector.tensor_copy(note_bf[:, :, 2 + s], note_tables[1][:, s, :].indirect(idx2[:]))
        note_words = sb.tile([P, J], U32, name="note_words", tag="note_words", align_bytes=ALIGN)
        note_bytes = sb.tile([P, J], U8, name="note_bytes", align_bytes=ALIGN)
        nc.vector.quantize_mx(note_words[:].bitcast(FP8X4), note_bytes[:], note_bf[:].rearrange("p j t -> p (j t)"))

        key_words = sb.tile([P, I], U32, name="key_words", tag="notes1", align_bytes=ALIGN)
        nc.vector.tensor_copy(key_words[:].rearrange("p (t s) -> p s t", t=PLACES), key_table[:].indirect(idx[:]))

        gain_picked = sb.tile([P, J], F32, name="gain_picked")
        nc.scalar.activation(gain_picked[:], gain_table[:].indirect(idx3[:]), ACT.Copy)
        gain_turned = ps.tile([P, HALVES, P], F32, name="gain_turned")
        for h in range(HALVES):
            nc.tensor.transpose(gain_turned[:, h, :], gain_picked[:, h * P : (h + 1) * P], ident[:])
        gain_column = sb.tile([P, HALVES], F32, name="gain_column")
        nc.scalar.copy(gain_column[:], gain_turned[:, :, 0])
        gain_spread = ps.tile([P, HALVES, P], F32, name="gain_spread")
        for h in range(HALVES):
            nc.tensor.transpose(gain_spread[:, h, :], gain_column[:, h : h + 1].to_broadcast([P, P]), ident[:])
        gain = sb.tile([P, J], F32, name="gain", tag="gain", align_bytes=ALIGN)
        nc.scalar.copy(gain[:], gain_spread[:].rearrange("p h j -> p (h j)"))

        gr1_words = sb.tile([P, J], U32, name="gr1_words", align_bytes=ALIGN)
        gr1_bytes = sb.tile([P, J], U8, name="gr1_bytes", align_bytes=ALIGN)
        g0 = sb.tile([P, J, PLACES], F32, name="g0")
        for h in range(HALVES):
            cols = slice(h * P, (h + 1) * P)
            g9 = ps.tile([P, PLACES, P], F32, name=f"g9_half{h}")
            for t in range(PLACES):
                rows = slice(t * P, (t + 1) * P)
                nc.tensor.matmul_mx(
                    g9[:, t, :],
                    lhsT=key_words[:, rows].bitcast(FP8X4),
                    lhsT_scale=key_bytes[:, rows],
                    rhs=note_words[:, cols].bitcast(FP8X4),
                    rhs_scale=note_bytes[:, cols],
                    start=True,
                    stop=True,
                )
            nc.scalar.activation(g0[:, cols, :], g9[:].rearrange("p t j -> p j t"), ACT.Tanh)
        gr1_bf = sb.tile([P, J, PLACES], BF16, name="gr1_bf", tag="vals0", align_bytes=ALIGN)
        nc.vector.tensor_tensor(gr1_bf[:], g0[:], row_factor[:].unsqueeze(1).to_broadcast([P, J, PLACES]), ALU.mult)
        nc.vector.quantize_mx(gr1_words[:].bitcast(FP8X4), gr1_bytes[:], gr1_bf[:].rearrange("p j t -> p (j t)"))

        def turn(picked, turned, copy):
            pairs = picked[:].bitcast(F32)
            bank = ps2.tile([P, 2, P], F32, name="turn_bank")
            for u in range(2):
                nc.tensor.transpose(bank[:, u, :], pairs[:, u : I // 2 : 2], ident[:])
            copy(turned.bitcast(F32), bank[:].rearrange("p u c -> p c u"))

        def multiply(turned, count):
            val_words = sb.tile([P, count * P], U32, name="val_words", bufs=3, align_bytes=ALIGN)
            val_bytes = sb.tile([P, count * P], U8, name="val_bytes", bufs=3, align_bytes=ALIGN)
            nc.vector.quantize_mx(val_words[:].bitcast(FP8X4), val_bytes[:], turned)
            sums = ps2.tile([P, count, J], F32, name="sums")
            for n in range(count):
                nc.tensor.matmul_mx(
                    sums[:, n, :],
                    lhsT=val_words[:, n * P : (n + 1) * P].bitcast(FP8X4),
                    lhsT_scale=val_bytes[:, n * P : (n + 1) * P],
                    rhs=gr1_words[:].bitcast(FP8X4),
                    rhs_scale=gr1_bytes[:],
                    start=True,
                    stop=True,
                )
            return sums

        turned01 = shared.tile([P, 2, P, PLACES], BF16, name="turned01", offset=TURNED01_AT, align_bytes=ALIGN)
        picked0 = sb.tile([P, I], BF16, name="picked0", tag="keys", align_bytes=ALIGN)
        nc.vector.tensor_copy(picked0[:], val_tables[0][:].indirect(idx[:]))
        turn(picked0, turned01[:, 0], nc.vector.tensor_copy)
        picked1 = sb.tile([P, I], BF16, name="picked1", tag="note_words", align_bytes=ALIGN)
        nc.scalar.activation(picked1[:], val_tables[1][:].indirect(idx[:]), ACT.Copy)
        turn(picked1, turned01[:, 1], nc.vector.tensor_copy)
        sums01 = multiply(turned01[:].rearrange("p n c t -> p (n c t)"), 2)

        picked2 = sb.tile([P, I], BF16, name="picked2", tag="vals1", align_bytes=ALIGN)
        nc.scalar.activation(picked2[:], val_tables[2][:].indirect(idx[:]), ACT.Copy)
        picked3 = shared.tile([P, I], BF16, name="picked3", offset=PICKED3_AT, align_bytes=ALIGN)
        cut = LAST_VALUES_ON_VECTOR
        nc.vector.tensor_copy(picked3[:, :cut], val_tables[3][:].indirect(idx[:, : cut // PER_COLUMN]))
        nc.scalar.activation(picked3[:, cut:], val_tables[3][:].indirect(idx[:, cut // PER_COLUMN :]), ACT.Copy)
        gained01 = shared.tile([P, 2, J], F32, name="gained01", offset=GAINED01_AT, align_bytes=ALIGN)
        nc.vector.tensor_tensor(gained01[:], sums01[:], gain[:].unsqueeze(1).to_broadcast([P, 2, J]), ALU.mult)
        turned2 = shared.tile([P, P, PLACES], BF16, name="turned2", offset=TURNED2_AT, align_bytes=ALIGN)
        turn(picked2, turned2[:], nc.scalar.copy)
        sums2 = multiply(turned2[:].rearrange("p c t -> p (c t)"), 1)
        turned3 = sb.tile([P, P, PLACES], BF16, name="turned3", tag="turned3", align_bytes=ALIGN)
        turn(picked3, turned3[:], nc.vector.tensor_copy)
        sums3 = multiply(turned3[:].rearrange("p c t -> p (c t)"), 1)

        looked = [
            shared.tile([P, J], F32, name="looked0", offset=LOOKED0_AT, align_bytes=ALIGN),
            sb.tile([P, J], F32, name="looked1", tag="held0", align_bytes=ALIGN),
            sb.tile([P, J - MERGE2_ON_VECTOR], F32, name="looked2", tag="held1", align_bytes=ALIGN),
        ]
        for b in range(2):
            nc.scalar.activation(looked[b][:], held_tables[b][:].indirect(idx3[:]), ACT.Copy)
        split = MERGE2_ON_VECTOR
        nc.scalar.activation(looked[2][:], held_tables[2][:].indirect(idx3[:, split // PER_COLUMN :]), ACT.Copy)
        after_last_quantise = sb.tile([P, 3, J], F32, name="after_last_quantise", tag="turned3", align_bytes=ALIGN)
        result01 = after_last_quantise[:, 0:2, :]
        gained2 = after_last_quantise[:, 2, :]
        nc.vector.tensor_tensor(gained2, sums2[:, 0, :], gain[:], ALU.mult)
        gained3 = sb.tile([P, J], F32, name="gained3")
        nc.vector.tensor_tensor(gained3[:], sums3[:, 0, :], gain[:], ALU.mult)
        for b in range(2):
            nc.vector.tensor_tensor(result01[:, b, :], looked[b][:], gained01[:, b, :], ALU.add)
        nc.sync.dma_start(out_by_block[:, 0:2, :], result01)
        result2 = sb.tile([P, J], F32, name="result2", tag="gain", align_bytes=ALIGN)
        nc.vector.tensor_tensor(
            result2[:, :split], held_tables[2][:].indirect(idx3[:, : split // PER_COLUMN]), gained2[:, :split], ALU.add
        )
        nc.vector.tensor_tensor(result2[:, split:], looked[2][:], gained2[:, split:], ALU.add)
        nc.sync.dma_start(out_by_block[:, 2, :], result2[:])
        result3 = sb.tile([P, J], F32, name="result3", tag="held1", align_bytes=ALIGN)
        nc.vector.tensor_tensor(result3[:], held_tables[3][:].indirect(idx3[:]), gained3[:], ALU.add)
        nc.sync.dma_start(out_by_block[:, 3, :], result3[:])
